import numpy as np
import ml_dtypes


def mxq(x, axis, fmt="e4m3"):
    dtype, down = {"e4m3": (ml_dtypes.float8_e4m3fn, 7), "e5m2": (ml_dtypes.float8_e5m2, 14)}[fmt]
    v = np.moveaxis(np.asarray(x, np.float32).astype(ml_dtypes.bfloat16).astype(np.float64), axis, -1)
    blocks = v.reshape(v.shape[:-1] + (-1, 32))
    amax = np.abs(blocks).max(-1, keepdims=True)
    byte = np.maximum(np.where(amax > 0, np.frexp(amax)[1] - 1 + 127, 0) - down, 1)
    scale = np.exp2(byte - 127.0)
    codes = (blocks / scale).astype(np.float32).astype(dtype).astype(np.float64)
    return np.moveaxis((codes * scale).reshape(v.shape), -1, axis)


WIDE = False


def mx_kscale(k):
    if not WIDE:
        return np.ones(k)
    levels = np.array([30, -30])
    if k % 512:
        return np.exp2(np.random.permutation(np.resize(levels, k // 32))).repeat(32)
    a = np.empty((k // 512, 16))
    for p in range(k // 512):
        a[p, :8] = np.random.permutation(np.resize(levels, 8))
        for g in range(8):
            far = levels[np.abs(levels - a[p, g]) >= 10]
            a[p, g + 8] = far[np.random.randint(len(far))]
    return np.exp2(a.ravel()).repeat(32)


def f64(x):
    return np.asarray(x).astype(np.float64)


def striped(idx):
    return np.tile(np.asarray(idx).reshape(-1, 16).T, (8, 1)).astype(np.uint16)


def unstriped(offs):
    return offs[:16].T.reshape(-1).astype(np.int64)


E2M1 = np.array([0.0, 0.5, 1.0, 1.5, 2.0, 3.0, 4.0, 6.0, -0.0, -0.5, -1.0, -1.5, -2.0, -3.0, -4.0, -6.0])


def pack_weight(w, fmt):
    k, n = w.shape
    w = f64(np.asarray(w, np.float32).astype(ml_dtypes.bfloat16)).reshape(k // 32, 32, n)
    amax = np.abs(w).max(1)
    if fmt == "e4m3":
        byte = np.frexp(amax)[1] - 1 + 127 - 7
    else:
        mant, ex = np.frexp(amax / 6.0)
        byte = np.where(mant > 0.5, ex, ex - 1) + 127
    byte = np.clip(np.where(amax > 0, byte, 1), 1, 254)
    scaled = (w * np.exp2(127.0 - byte)[:, None, :]).reshape(k, n).astype(np.float32)
    by_word = np.ascontiguousarray(scaled.reshape(k // 512, 128, 4, n).transpose(0, 1, 3, 2))
    if fmt == "e4m3":
        words = by_word.astype(ml_dtypes.float8_e4m3fn).view(np.uint8)
    else:
        c = by_word.astype(ml_dtypes.float4_e2m1fn).view(np.uint8) & 0xF
        words = (c[..., 0::2] | (c[..., 1::2] << 4)).reshape(k // 512, 128, 2 * n)
    return np.ascontiguousarray(words), np.ascontiguousarray(byte.astype(np.uint8).reshape(k // 512, 16, n))


def unpack_weight(words, scales, fmt):
    g, _, n = scales.shape
    words = np.ascontiguousarray(words).reshape(g, 128, n, -1)
    if fmt == "e4m3":
        vals = words.view(ml_dtypes.float8_e4m3fn).astype(np.float64)
    else:
        nib = np.empty((g, 128, n, 4), np.uint8)
        nib[..., 0::2] = words & 0xF
        nib[..., 1::2] = words >> 4
        vals = E2M1[nib]
    vals = vals * np.repeat(np.exp2(scales.astype(np.float64) - 127.0), 8, axis=1)[..., None]
    return vals.transpose(0, 1, 3, 2).reshape(g * 512, n)


K, T, J, R, O, N, Z = 512, 512, 256, 512, 128, 256, 512


def setup_inputs():
    n = np.random.standard_normal
    idx = np.random.permutation(T)[:J]
    idx2 = np.random.permutation(J)[:O]
    idx3 = np.random.permutation(J)[:O]
    idx4 = np.random.permutation(Z)[:O]
    fk = mx_kscale(K)
    fr = mx_kscale(R)
    wp = pack_weight(n((K, R)) * 1 / np.sqrt(K) * fk[:, None] * fr, "e2m1")
    wbp = pack_weight(n((R, N)) * 1 / np.sqrt(R) / fr[:, None], "e4m3")
    return {
        "xf": (n((K, T))).astype(np.float32),
        "ow": (n((K, J)) * 0.7).astype(np.float32),
        "fk": (np.random.uniform(0.5, 2.0, (K, 1)) / fk[:, None]).astype(np.float32),
        "w_words": wp[0],
        "w_scales": wp[1],
        "wb_words": wbp[0],
        "wb_scales": wbp[1],
        "tz": (n((N, Z))).astype(np.float32),
        "offs": striped(idx),
        "offs2": striped(idx2),
        "offs3": striped(idx3),
        "offs4": striped(idx4),
    }


def reference(xf, ow, fk, w_words, w_scales, wb_words, wb_scales, tz, offs, offs2, offs3, offs4):
    idx = unstriped(offs)
    idx2 = unstriped(offs2)
    idx3 = unstriped(offs3)
    idx4 = unstriped(offs4)
    wu = unpack_weight(w_words, w_scales, "e2m1")
    wbu = unpack_weight(wb_words, wb_scales, "e4m3")
    u = (f64(xf)[:, idx] - f64(ow)) * f64(fk)
    uq = mxq(u, 0, "e4m3")
    a = wu.T @ uq
    hid = np.maximum(a[:, idx2], a[:, idx3])
    hidq = mxq(hid, 0, "e5m2")
    p = wbu.T @ hidq
    y = p * f64(tz)[:, idx4]
    return y

@@ -1,0 +1,157 @@
+from contextlib import ExitStack
+
+import concourse.mybir as mybir
+
+K, T, J, R, O, N, Z = 512, 512, 256, 512, 128, 256, 512
+FLOPS = 2 * K * R * J + 2 * R * N * O
+
+F32 = mybir.dt.float32
+BF16 = mybir.dt.bfloat16
+I32 = mybir.dt.int32
+U32 = mybir.dt.uint32
+U16 = mybir.dt.uint16
+U8 = mybir.dt.uint8
+E4M3 = mybir.dt.float8_e4m3fn_x4
+E5M2 = mybir.dt.float8_e5m2_x4
+E2M1 = mybir.dt.float4_e2m1fn_x4
+ALU = mybir.AluOpType
+COPY = mybir.ActivationFunctionType.Copy
+
+P = 128
+PACK = 4
+
+
+def tile_list_looks_offsetpicks_larger_timeslook_kernel(
+    tc, xf, ow, fk, w_words, w_scales, wb_words, wb_scales, tz, offs, offs2, offs3, offs4, out
+):
+    nc = tc.nc
+    with ExitStack() as ctx:
+        sb = ctx.enter_context(tc.tile_pool(name="sb", bufs=1))
+        ps = ctx.enter_context(tc.psum_pool(name="ps", bufs=1))
+
+        list1 = sb.tile([P, J // 16], U16, name="list1")
+        list2 = sb.tile([P, O // 16], U16, name="list2")
+        list3 = sb.tile([P, O // 16], U16, name="list3")
+        list4 = sb.tile([P, O // 16], U16, name="list4")
+        fk_sb = sb.tile([P, PACK], F32, name="fk_sb")
+        ow_sb = [sb.tile([P, 2, J], F32, name="ow_sb%d" % i) for i in range(2)]
+        x_sb = [sb.tile([P, T], F32, name="x_sb%d" % i) for i in range(PACK)]
+        w_raw = sb.tile([P, 2 * R], U8, name="w_raw", align_bytes=64)
+        ws_raw = sb.tile([P, R], U8, name="ws_raw", align_bytes=64)
+        w_sb = sb.tile([P, 2 * R], U8, name="w_sb", align_bytes=64)
+        ws_sb = sb.tile([P, R], U8, name="ws_sb", align_bytes=64)
+        wb_sb = sb.tile([P, N], U32, name="wb_sb", align_bytes=64)
+        wbs_sb = sb.tile([P, N], U8, name="wbs_sb", align_bytes=64)
+        tz_sb = sb.tile([P, 2, Z], F32, name="tz_sb")
+
+        nc.vector.memset(ws_raw[:].bitcast(I32), 0)
+        nc.vector.memset(wbs_sb[:].bitcast(I32), 0)
+
+        nc.sync.dma_start(list1[:], offs)
+        nc.scalar.dma_start(fk_sb[:], fk.rearrange("(p i) o -> p (i o)", i=PACK))
+        for q in range(4):
+            nc.scalar.dma_start(
+                ws_raw[32 * q : 32 * q + 4, :].bitcast(I32), w_scales[0, 4 * q : 4 * q + 4, :].bitcast(I32)
+            )
+        x_rows = xf.rearrange("(p i) t -> p i t", i=PACK)
+        ow_rows = ow.rearrange("(p i) j -> p i j", i=PACK)
+        for i in range(PACK):
+            if i % 2 == 0:
+                nc.sync.dma_start(ow_sb[i // 2][:], ow_rows[:, i : i + 2, :])
+            nc.sync.dma_start(x_sb[i][:], x_rows[:, i, :])
+        nc.sync.dma_start(w_raw[:].bitcast(I32), w_words[0].bitcast(I32))
+        nc.sync.dma_start(list2[:], offs2)
+        nc.sync.dma_start(list3[:], offs3)
+        nc.sync.dma_start(list4[:], offs4)
+        nc.sync.dma_start(tz_sb[:], tz.rearrange("(h p) z -> p h z", p=P))
+        nc.sync.dma_start(wb_sb[:].bitcast(I32), wb_words[0].rearrange("p n t -> p (n t)").bitcast(I32))
+        for q in range(4):
+            nc.sync.dma_start(
+                wbs_sb[32 * q : 32 * q + 4, :].bitcast(I32), wb_scales[0, 4 * q : 4 * q + 4, :].bitcast(I32)
+            )
+
+        nc.vector.tensor_copy(
+            ws_sb[:].rearrange("p (t m) -> p t m", t=PACK),
+            ws_raw[:].rearrange("p (m t) -> p t m", t=PACK),
+        )
+
+        H = J // 2
+        diff = sb.tile([P, PACK, J], F32, name="diff")
+        diff_last = sb.tile([P, H], F32, name="diff_last")
+        u_bf = [sb.tile([P, H * PACK], BF16, name="u_bf%d" % h, align_bytes=64) for h in range(2)]
+        u_lo = u_bf[0][:].rearrange("p (j i) -> p i j", i=PACK)
+        for i in range(PACK - 1):
+            nc.vector.tensor_tensor(
+                diff[:, i, :], x_sb[i][:].indirect(list1[:]), ow_sb[i // 2][:, i % 2, :], ALU.subtract
+            )
+            nc.scalar.activation(u_lo[:, i, :], diff[:, i, 0:H], COPY, scale=fk_sb[:, i : i + 1])
+        nc.vector.tensor_tensor(diff[:, 3, H:J], x_sb[3][:].indirect(list1[:, 8:16]), ow_sb[1][:, 1, H:J], ALU.subtract)
+        nc.vector.tensor_tensor(diff_last[:], x_sb[3][:].indirect(list1[:, 0:8]), ow_sb[1][:, 1, 0:H], ALU.subtract)
+        nc.scalar.activation(u_lo[:, 3, :], diff_last[:], COPY, scale=fk_sb[:, 3:4])
+        nc.vector.tensor_tensor(
+            u_bf[1][:].rearrange("p (c e i) -> p c i e", e=4, i=PACK),
+            diff[:, :, H:J].rearrange("p i (c e) -> p c i e", e=4),
+            fk_sb[:].unsqueeze(1).unsqueeze(3).to_broadcast([P, H // 4, PACK, 4]),
+            ALU.mult,
+        )
+        u_q = sb.tile([P, J], U32, name="u_q", align_bytes=64)
+        u_s = sb.tile([P, J], U8, name="u_s", align_bytes=64)
+        for h in (1, 0):
+            nc.vector.quantize_mx(
+                out=u_q[:, h * H : (h + 1) * H].bitcast(E4M3), scales=u_s[:, h * H : (h + 1) * H], in_=u_bf[h][:]
+            )
+        nc.vector.tensor_copy(
+            w_sb[:].bitcast(U16).rearrange("p (t m) -> p t m", t=PACK),
+            w_raw[:].bitcast(U16).rearrange("p (m t) -> p t m", t=PACK),
+        )
+
+        a_ps = [ps.tile([P, J], F32, name="a_ps%d" % t) for t in range(PACK)]
+        a_sb = [sb.tile([P, J], F32, name="a_sb%d" % t, tag="a_sb%d" % t) for t in range(PACK)]
+        for t in range(PACK):
+            nc.tensor.matmul_mx(
+                out=a_ps[t][:],
+                lhsT=w_sb[:, 2 * P * t : 2 * P * (t + 1)].bitcast(E2M1),
+                lhsT_scale=ws_sb[:, P * t : P * (t + 1)],
+                rhs=u_q[:].bitcast(E4M3),
+                rhs_scale=u_s[:],
+                start=True,
+                stop=True,
+            )
+        pick2 = sb.tile([P, PACK, O], F32, name="pick2")
+        pick3 = sb.tile([P, PACK, O], F32, name="pick3")
+        for t in range(PACK):
+            if t % 2 == 0:
+                nc.scalar.copy(a_sb[t][:], a_ps[t][:])
+            else:
+                nc.vector.tensor_copy(a_sb[t][:], a_ps[t][:])
+        for t in range(PACK):
+            nc.vector.tensor_copy(pick2[:, t, :], a_sb[t][:].indirect(list2[:]))
+            nc.scalar.activation(pick3[:, t, :], a_sb[t][:].indirect(list3[:]), COPY)
+        tz_pick = sb.tile([P, 2, O], F32, name="tz_pick", tag="a_sb3")
+        for h in range(2):
+            nc.scalar.activation(tz_pick[:, h, :], tz_sb[:, h, :].indirect(list4[:]), COPY)
+        h_bf = sb.tile([P, O * PACK], BF16, name="h_bf", align_bytes=64)
+        nc.vector.tensor_tensor(
+            h_bf[:].rearrange("p (c e t) -> p c t e", e=4, t=PACK),
+            pick2[:].rearrange("p t (c e) -> p c t e", e=4),
+            pick3[:].rearrange("p t (c e) -> p c t e", e=4),
+            ALU.max,
+        )
+        h_q = sb.tile([P, O], U32, name="h_q", align_bytes=64)
+        h_s = sb.tile([P, O], U8, name="h_s", align_bytes=64)
+        nc.vector.quantize_mx(out=h_q[:].bitcast(E5M2), scales=h_s[:], in_=h_bf[:])
+
+        for h in range(2):
+            p_ps = ps.tile([P, O], F32, name="p_ps%d" % h)
+            nc.tensor.matmul_mx(
+                out=p_ps[:],
+                lhsT=wb_sb[:, P * h : P * (h + 1)].bitcast(E4M3),
+                lhsT_scale=wbs_sb[:, P * h : P * (h + 1)],
+                rhs=h_q[:].bitcast(E5M2),
+                rhs_scale=h_s[:],
+                start=True,
+                stop=True,
+            )
+            y_sb = sb.tile([P, O], F32, name="y_sb%d" % h)
+            nc.vector.tensor_tensor(y_sb[:], p_ps[:], tz_pick[:, h, :], ALU.mult)
+            (nc.sync if h == 0 else nc.scalar).dma_start(out[P * h : P * (h + 1), :], y_sb[:])

@@ -44,12 +44,17 @@ def tile_list_looks_offsetpicks_larger_timeslook_kernel(
         wbs_sb = sb.tile([P, N], U8, name="wbs_sb", align_bytes=64)
         tz_sb = sb.tile([P, 2, Z], F32, name="tz_sb")
 
-        nc.vector.memset(ws_raw[:].bitcast(I32), 0)
+        nc.vector.memset(ws_raw[32:64, :].bitcast(I32), 0)
+        nc.vector.memset(ws_raw[64:128, :].bitcast(I32), 0)
         nc.vector.memset(wbs_sb[:].bitcast(I32), 0)
 
         nc.sync.dma_start(list1[:], offs)
         nc.scalar.dma_start(fk_sb[:], fk.rearrange("(p i) o -> p (i o)", i=PACK))
-        for q in range(4):
+        nc.scalar.dma_start(
+            ws_raw[0:32, :].bitcast(I32),
+            w_scales[0, 0:4, :].bitcast(I32).unsqueeze(0).to_broadcast([8, 4, R // 4]),
+        )
+        for q in range(1, 4):
             nc.scalar.dma_start(
                 ws_raw[32 * q : 32 * q + 4, :].bitcast(I32), w_scales[0, 4 * q : 4 * q + 4, :].bitcast(I32)
             )
@@ -105,44 +110,49 @@ def tile_list_looks_offsetpicks_larger_timeslook_kernel(
             w_raw[:].bitcast(U16).rearrange("p (m t) -> p t m", t=PACK),
         )
 
-        a_ps = [ps.tile([P, J], F32, name="a_ps%d" % t) for t in range(PACK)]
         a_sb = [sb.tile([P, J], F32, name="a_sb%d" % t, tag="a_sb%d" % t) for t in range(PACK)]
+        a_ps = {}
         for t in range(PACK):
-            nc.tensor.matmul_mx(
-                out=a_ps[t][:],
-                lhsT=w_sb[:, 2 * P * t : 2 * P * (t + 1)].bitcast(E2M1),
-                lhsT_scale=ws_sb[:, P * t : P * (t + 1)],
-                rhs=u_q[:].bitcast(E4M3),
-                rhs_scale=u_s[:],
-                start=True,
-                stop=True,
-            )
+            for h in (1, 0):
+                a_ps[t, h] = ps.tile([P, H], F32, name="a_ps%d%d" % (t, h), tag="bank%d" % (2 * t + h))
+                nc.tensor.matmul_mx(
+                    out=a_ps[t, h][:],
+                    lhsT=w_sb[:, 2 * P * t : 2 * P * (t + 1)].bitcast(E2M1),
+                    lhsT_scale=ws_sb[:, P * t : P * (t + 1)],
+                    rhs=u_q[:, h * H : (h + 1) * H].bitcast(E4M3),
+                    rhs_scale=u_s[:, h * H : (h + 1) * H],
+                    start=True,
+                    stop=True,
+                )
         pick2 = sb.tile([P, PACK, O], F32, name="pick2")
         pick3 = sb.tile([P, PACK, O], F32, name="pick3")
         for t in range(PACK):
-            if t % 2 == 0:
-                nc.scalar.copy(a_sb[t][:], a_ps[t][:])
-            else:
-                nc.vector.tensor_copy(a_sb[t][:], a_ps[t][:])
+            nc.scalar.copy(a_sb[t][:, H:J], a_ps[t, 1][:])
+            nc.vector.tensor_copy(a_sb[t][:, 0:H], a_ps[t, 0][:])
         for t in range(PACK):
             nc.vector.tensor_copy(pick2[:, t, :], a_sb[t][:].indirect(list2[:]))
             nc.scalar.activation(pick3[:, t, :], a_sb[t][:].indirect(list3[:]), COPY)
         tz_pick = sb.tile([P, 2, O], F32, name="tz_pick", tag="a_sb3")
         for h in range(2):
             nc.scalar.activation(tz_pick[:, h, :], tz_sb[:, h, :].indirect(list4[:]), COPY)
-        h_bf = sb.tile([P, O * PACK], BF16, name="h_bf", align_bytes=64)
-        nc.vector.tensor_tensor(
-            h_bf[:].rearrange("p (c e t) -> p c t e", e=4, t=PACK),
-            pick2[:].rearrange("p t (c e) -> p c t e", e=4),
-            pick3[:].rearrange("p t (c e) -> p c t e", e=4),
-            ALU.max,
-        )
+        G = O // 2
+        h_bf = [sb.tile([P, G * PACK], BF16, name="h_bf%d" % g, align_bytes=64) for g in range(2)]
+        for g in range(2):
+            nc.vector.tensor_tensor(
+                h_bf[g][:].rearrange("p (c e t) -> p c t e", e=4, t=PACK),
+                pick2[:, :, g * G : (g + 1) * G].rearrange("p t (c e) -> p c t e", e=4),
+                pick3[:, :, g * G : (g + 1) * G].rearrange("p t (c e) -> p c t e", e=4),
+                ALU.max,
+            )
         h_q = sb.tile([P, O], U32, name="h_q", align_bytes=64)
         h_s = sb.tile([P, O], U8, name="h_s", align_bytes=64)
-        nc.vector.quantize_mx(out=h_q[:].bitcast(E5M2), scales=h_s[:], in_=h_bf[:])
+        for g in range(2):
+            nc.vector.quantize_mx(
+                out=h_q[:, g * G : (g + 1) * G].bitcast(E5M2), scales=h_s[:, g * G : (g + 1) * G], in_=h_bf[g][:]
+            )
 
         for h in range(2):
-            p_ps = ps.tile([P, O], F32, name="p_ps%d" % h)
+            p_ps = ps.tile([P, O], F32, name="p_ps%d" % h, tag="bank%d" % h)
             nc.tensor.matmul_mx(
                 out=p_ps[:],
                 lhsT=wb_sb[:, P * h : P * (h + 1)].bitcast(E4M3),

from contextlib import ExitStack

import concourse.mybir as mybir

K, T, J, R, O, N, Z = 512, 512, 256, 512, 128, 256, 512
FLOPS = 2 * K * R * J + 2 * R * N * O

F32 = mybir.dt.float32
BF16 = mybir.dt.bfloat16
I32 = mybir.dt.int32
U32 = mybir.dt.uint32
U16 = mybir.dt.uint16
U8 = mybir.dt.uint8
E4M3 = mybir.dt.float8_e4m3fn_x4
E5M2 = mybir.dt.float8_e5m2_x4
E2M1 = mybir.dt.float4_e2m1fn_x4
ALU = mybir.AluOpType
COPY = mybir.ActivationFunctionType.Copy

P = 128
PACK = 4


def tile_list_looks_offsetpicks_larger_timeslook_kernel(
    tc, xf, ow, fk, w_words, w_scales, wb_words, wb_scales, tz, offs, offs2, offs3, offs4, out
):
    nc = tc.nc
    with ExitStack() as ctx:
        sb = ctx.enter_context(tc.tile_pool(name="sb", bufs=1))
        ps = ctx.enter_context(tc.psum_pool(name="ps", bufs=1))

        list1 = sb.tile([P, J // 16], U16, name="list1")
        list2 = sb.tile([P, O // 16], U16, name="list2")
        list3 = sb.tile([P, O // 16], U16, name="list3")
        list4 = sb.tile([P, O // 16], U16, name="list4")
        fk_sb = sb.tile([P, PACK], F32, name="fk_sb")
        ow_sb = [sb.tile([P, 2, J], F32, name="ow_sb%d" % i) for i in range(2)]
        x_sb = [sb.tile([P, T], F32, name="x_sb%d" % i) for i in range(PACK)]
        w_raw = sb.tile([P, 2 * R], U8, name="w_raw", align_bytes=64)
        ws_raw = sb.tile([P, R], U8, name="ws_raw", align_bytes=64)
        w_sb = sb.tile([P, 2 * R], U8, name="w_sb", align_bytes=64)
        ws_sb = sb.tile([P, R], U8, name="ws_sb", align_bytes=64)
        wb_sb = sb.tile([P, N], U32, name="wb_sb", align_bytes=64)
        wbs_sb = sb.tile([P, N], U8, name="wbs_sb", align_bytes=64)
        tz_sb = sb.tile([P, 2, Z], F32, name="tz_sb")

        nc.vector.memset(ws_raw[32:64, :].bitcast(I32), 0)
        nc.vector.memset(ws_raw[64:128, :].bitcast(I32), 0)
        nc.vector.memset(wbs_sb[:].bitcast(I32), 0)

        nc.sync.dma_start(list1[:], offs)
        nc.scalar.dma_start(fk_sb[:], fk.rearrange("(p i) o -> p (i o)", i=PACK))
        nc.scalar.dma_start(
            ws_raw[0:32, :].bitcast(I32),
            w_scales[0, 0:4, :].bitcast(I32).unsqueeze(0).to_broadcast([8, 4, R // 4]),
        )
        for q in range(1, 4):
            nc.scalar.dma_start(
                ws_raw[32 * q : 32 * q + 4, :].bitcast(I32), w_scales[0, 4 * q : 4 * q + 4, :].bitcast(I32)
            )
        x_rows = xf.rearrange("(p i) t -> p i t", i=PACK)
        ow_rows = ow.rearrange("(p i) j -> p i j", i=PACK)
        for i in range(PACK):
            if i % 2 == 0:
                nc.sync.dma_start(ow_sb[i // 2][:], ow_rows[:, i : i + 2, :])
            nc.sync.dma_start(x_sb[i][:], x_rows[:, i, :])
        nc.sync.dma_start(w_raw[:].bitcast(I32), w_words[0].bitcast(I32))
        nc.sync.dma_start(list2[:], offs2)
        nc.sync.dma_start(list3[:], offs3)
        nc.sync.dma_start(list4[:], offs4)
        nc.sync.dma_start(tz_sb[:], tz.rearrange("(h p) z -> p h z", p=P))
        nc.sync.dma_start(wb_sb[:].bitcast(I32), wb_words[0].rearrange("p n t -> p (n t)").bitcast(I32))
        for q in range(4):
            nc.sync.dma_start(
                wbs_sb[32 * q : 32 * q + 4, :].bitcast(I32), wb_scales[0, 4 * q : 4 * q + 4, :].bitcast(I32)
            )

        nc.vector.tensor_copy(
            ws_sb[:].rearrange("p (t m) -> p t m", t=PACK),
            ws_raw[:].rearrange("p (m t) -> p t m", t=PACK),
        )

        H = J // 2
        diff = sb.tile([P, PACK, J], F32, name="diff")
        diff_last = sb.tile([P, H], F32, name="diff_last")
        u_bf = [sb.tile([P, H * PACK], BF16, name="u_bf%d" % h, align_bytes=64) for h in range(2)]
        u_lo = u_bf[0][:].rearrange("p (j i) -> p i j", i=PACK)
        for i in range(PACK - 1):
            nc.vector.tensor_tensor(
                diff[:, i, :], x_sb[i][:].indirect(list1[:]), ow_sb[i // 2][:, i % 2, :], ALU.subtract
            )
            nc.scalar.activation(u_lo[:, i, :], diff[:, i, 0:H], COPY, scale=fk_sb[:, i : i + 1])
        nc.vector.tensor_tensor(diff[:, 3, H:J], x_sb[3][:].indirect(list1[:, 8:16]), ow_sb[1][:, 1, H:J], ALU.subtract)
        nc.vector.tensor_tensor(diff_last[:], x_sb[3][:].indirect(list1[:, 0:8]), ow_sb[1][:, 1, 0:H], ALU.subtract)
        nc.scalar.activation(u_lo[:, 3, :], diff_last[:], COPY, scale=fk_sb[:, 3:4])
        nc.vector.tensor_tensor(
            u_bf[1][:].rearrange("p (c e i) -> p c i e", e=4, i=PACK),
            diff[:, :, H:J].rearrange("p i (c e) -> p c i e", e=4),
            fk_sb[:].unsqueeze(1).unsqueeze(3).to_broadcast([P, H // 4, PACK, 4]),
            ALU.mult,
        )
        u_q = sb.tile([P, J], U32, name="u_q", align_bytes=64)
        u_s = sb.tile([P, J], U8, name="u_s", align_bytes=64)
        for h in (1, 0):
            nc.vector.quantize_mx(
                out=u_q[:, h * H : (h + 1) * H].bitcast(E4M3), scales=u_s[:, h * H : (h + 1) * H], in_=u_bf[h][:]
            )
        nc.vector.tensor_copy(
            w_sb[:].bitcast(U16).rearrange("p (t m) -> p t m", t=PACK),
            w_raw[:].bitcast(U16).rearrange("p (m t) -> p t m", t=PACK),
        )

        a_sb = [sb.tile([P, J], F32, name="a_sb%d" % t, tag="a_sb%d" % t) for t in range(PACK)]
        a_ps = {}
        for t in range(PACK):
            for h in (1, 0):
                a_ps[t, h] = ps.tile([P, H], F32, name="a_ps%d%d" % (t, h), tag="bank%d" % (2 * t + h))
                nc.tensor.matmul_mx(
                    out=a_ps[t, h][:],
                    lhsT=w_sb[:, 2 * P * t : 2 * P * (t + 1)].bitcast(E2M1),
                    lhsT_scale=ws_sb[:, P * t : P * (t + 1)],
                    rhs=u_q[:, h * H : (h + 1) * H].bitcast(E4M3),
                    rhs_scale=u_s[:, h * H : (h + 1) * H],
                    start=True,
                    stop=True,
                )
        pick2 = sb.tile([P, PACK, O], F32, name="pick2")
        pick3 = sb.tile([P, PACK, O], F32, name="pick3")
        for t in range(PACK):
            nc.scalar.copy(a_sb[t][:, H:J], a_ps[t, 1][:])
            nc.vector.tensor_copy(a_sb[t][:, 0:H], a_ps[t, 0][:])
        for t in range(PACK):
            nc.vector.tensor_copy(pick2[:, t, :], a_sb[t][:].indirect(list2[:]))
            nc.scalar.activation(pick3[:, t, :], a_sb[t][:].indirect(list3[:]), COPY)
        tz_pick = sb.tile([P, 2, O], F32, name="tz_pick", tag="a_sb3")
        for h in range(2):
            nc.scalar.activation(tz_pick[:, h, :], tz_sb[:, h, :].indirect(list4[:]), COPY)
        G = O // 2
        h_bf = [sb.tile([P, G * PACK], BF16, name="h_bf%d" % g, align_bytes=64) for g in range(2)]
        for g in range(2):
            nc.vector.tensor_tensor(
                h_bf[g][:].rearrange("p (c e t) -> p c t e", e=4, t=PACK),
                pick2[:, :, g * G : (g + 1) * G].rearrange("p t (c e) -> p c t e", e=4),
                pick3[:, :, g * G : (g + 1) * G].rearrange("p t (c e) -> p c t e", e=4),
                ALU.max,
            )
        h_q = sb.tile([P, O], U32, name="h_q", align_bytes=64)
        h_s = sb.tile([P, O], U8, name="h_s", align_bytes=64)
        for g in range(2):
            nc.vector.quantize_mx(
                out=h_q[:, g * G : (g + 1) * G].bitcast(E5M2), scales=h_s[:, g * G : (g + 1) * G], in_=h_bf[g][:]
            )

        for h in range(2):
            p_ps = ps.tile([P, O], F32, name="p_ps%d" % h, tag="bank%d" % h)
            nc.tensor.matmul_mx(
                out=p_ps[:],
                lhsT=wb_sb[:, P * h : P * (h + 1)].bitcast(E4M3),
                lhsT_scale=wbs_sb[:, P * h : P * (h + 1)],
                rhs=h_q[:].bitcast(E5M2),
                rhs_scale=h_s[:],
                start=True,
                stop=True,
            )
            y_sb = sb.tile([P, O], F32, name="y_sb%d" % h)
            nc.vector.tensor_tensor(y_sb[:], p_ps[:], tz_pick[:, h, :], ALU.mult)
            (nc.sync if h == 0 else nc.scalar).dma_start(out[P * h : P * (h + 1), :], y_sb[:])
